import numpy as np
import ml_dtypes


def mxq(x, axis, fmt="e4m3"):
    dtype, down = {"e4m3": (ml_dtypes.float8_e4m3fn, 7), "e5m2": (ml_dtypes.float8_e5m2, 14)}[fmt]
    v = np.moveaxis(np.asarray(x, np.float32).astype(ml_dtypes.bfloat16).astype(np.float64), axis, -1)
    blocks = v.reshape(v.shape[:-1] + (-1, 32))
    amax = np.abs(blocks).max(-1, keepdims=True)
    byte = np.maximum(np.where(amax > 0, np.frexp(amax)[1] - 1 + 127, 0) - down, 1)
    scale = np.exp2(byte - 127.0)
    codes = (blocks / scale).astype(np.float32).astype(dtype).astype(np.float64)
    return np.moveaxis((codes * scale).reshape(v.shape), -1, axis)


WIDE = False


def mx_kscale(k):
    if not WIDE:
        return np.ones(k)
    levels = np.array([10, -10, 5, -5, 0])
    if k % 512:
        return np.exp2(np.random.permutation(np.resize(levels, k // 32))).repeat(32)
    a = np.empty((k // 512, 16))
    for p in range(k // 512):
        a[p, :8] = np.random.permutation(np.resize(levels, 8))
        for g in range(8):
            far = levels[np.abs(levels - a[p, g]) >= 10]
            a[p, g + 8] = far[np.random.randint(len(far))]
    return np.exp2(a.ravel()).repeat(32)


def f64(x):
    return np.asarray(x).astype(np.float64)


def striped(idx):
    return np.tile(idx.reshape(-1, 16).T, (8, 1)).astype(np.uint16)


def unstriped(offs):
    return offs[:16].T.reshape(-1).astype(np.int64)


def striped8(idx):
    return np.concatenate([x.reshape(-1, 16).T for x in idx]).astype(np.uint16)


def runs(offs, k):
    lists = np.stack([offs[16 * r : 16 * r + 16].T.reshape(-1) for r in range(8)]).astype(np.int64)
    return lists[np.arange(k) % 512 // 64]


def pack_weight(w):
    k, n = w.shape
    w = f64(np.asarray(w, np.float32).astype(ml_dtypes.bfloat16)).reshape(k // 32, 32, n)
    amax = np.abs(w).max(1)
    byte = np.clip(np.where(amax > 0, np.frexp(amax)[1] - 1 + 127 - 7, 1), 1, 254)
    scaled = (w * np.exp2(127.0 - byte)[:, None, :]).reshape(k, n).astype(np.float32)
    words = np.ascontiguousarray(scaled.reshape(k // 512, 128, 4, n).transpose(0, 1, 3, 2)).astype(ml_dtypes.float8_e4m3fn).view(np.uint8)
    return words, np.ascontiguousarray(byte.astype(np.uint8).reshape(k // 512, 16, n))


def unpack_weight(words, scales):
    g, p, n, _ = words.shape
    vals = np.ascontiguousarray(words).view(ml_dtypes.float8_e4m3fn).astype(np.float64) * np.repeat(np.exp2(scales.astype(np.float64) - 127.0), 8, axis=1)[..., None]
    return vals.transpose(0, 1, 3, 2).reshape(g * 512, n)


K, T, S, G, H, W, C, U = 512, 1024, 512, 2048, 512, 256, 512, 1024


def setup_inputs():
    n = np.random.standard_normal
    s = mx_kscale(K)[:, None]
    packed_xT = pack_weight(n((K, T)) * s)
    packed_dT = pack_weight(n((K, G)) / s)
    perm = np.random.permutation(S)
    perm2 = np.random.permutation(S)
    perm3 = np.stack([np.random.permutation(U) for _ in range(8)])
    return {
        "x_words": packed_xT[0],
        "x_scales": packed_xT[1],
        "d_words": packed_dT[0],
        "d_scales": packed_dT[1],
        "gs": (np.random.uniform(0.5, 1.5, (K, 1)) / s).astype(np.float32),
        "offs": striped(np.random.permutation(T)[:S]),
        "k1": striped8(np.random.randint(0, G, (8, H))),
        "two": striped(np.random.permutation(T)[:S]),
        "k2": striped8(np.random.randint(0, G, (8, H))),
        "hz": striped8(np.random.randint(0, T, (8, S))),
        "k3": striped8(np.random.randint(0, G, (8, H))),
        "n1": striped(perm[:W]),
        "n2": striped(perm[W:]),
        "n3": striped(perm2[:W]),
        "n4": striped(perm2[W:]),
        "n5": striped(np.random.permutation(S)),
        "cand": striped8(np.random.randint(0, T, (8, C))),
        "n6": striped8(perm3[:, :S]),
        "n7": striped8(perm3[:, S:]),
        "n8": striped8(np.stack([np.random.permutation(S) for _ in range(8)])),
    }


def reference(x_words, x_scales, d_words, d_scales, gs, offs, k1, two, k2, hz, k3, n1, n2, n3, n4, n5, cand, n6, n7, n8):
    x_cand = unpack_weight(x_words, x_scales)[np.arange(K)[:, None], runs(cand, K)]
    d_k1 = unpack_weight(d_words, d_scales)[np.arange(K)[:, None], runs(k1, K)]
    xq = unpack_weight(x_words, x_scales)[:, unstriped(offs)]
    d_k2 = unpack_weight(d_words, d_scales)[np.arange(K)[:, None], runs(k2, K)]
    x_two = unpack_weight(x_words, x_scales)[:, unstriped(two)]
    d_k3 = unpack_weight(d_words, d_scales)[np.arange(K)[:, None], runs(k3, K)]
    x_hz = unpack_weight(x_words, x_scales)[np.arange(K)[:, None], runs(hz, K)]
    h = 0.0625 * (d_k1.T @ xq + d_k2.T @ x_two + d_k3.T @ x_hz)
    pa = h[:, unstriped(n1)]
    pb = h[:, unstriped(n2)]
    rb = np.maximum(pa, pb)
    ua = np.zeros((H, S))
    ua[:, unstriped(n3)] = pb
    ub = ua.copy()
    ub[:, unstriped(n4)] = rb
    z = f64(gs) * (ub - h[:, unstriped(n5)])
    s = 0.0625 * ((x_cand.T @ mxq(z, 0, "e4m3")))
    ds = np.zeros((C, S))
    ds[np.arange(C)[:, None], runs(n8, C)] = s
    up = np.maximum(s, ds)
    ph = np.zeros((C, U))
    ph[np.arange(C)[:, None], runs(n6, C)] = ds
    out = ph.copy()
    out[np.arange(C)[:, None], runs(n7, C)] = up
    return out

@@ -1,0 +1,211 @@
+from contextlib import ExitStack
+
+import concourse.mybir as mybir
+
+F32 = mybir.dt.float32
+BF16 = mybir.dt.bfloat16
+I32 = mybir.dt.int32
+U32 = mybir.dt.uint32
+U16 = mybir.dt.uint16
+U8 = mybir.dt.uint8
+FP8X4 = mybir.dt.float8_e4m3fn_x4
+ALU = mybir.AluOpType
+COPY = mybir.ActivationFunctionType.Copy
+
+P = 128
+PACK = 4
+T, G, S, W, U = 1024, 2048, 512, 256, 1024
+CHUNK = 128
+SIXTEENTH = 0.0625
+FLOPS = 4 * 2 * 512 * 512 * 512
+
+
+def tile_picked_mtthzkcpswpagsn_none_p_kernel(
+    tc, x_words, x_scales, d_words, d_scales, gs, offs, k1, two, k2, hz, k3,
+    n1, n2, n3, n4, n5, cand, n6, n7, n8, out,
+):
+    nc = tc.nc
+    with ExitStack() as ctx:
+        lists = ctx.enter_context(tc.tile_pool(name="lists", bufs=1))
+        keep = ctx.enter_context(tc.tile_pool(name="keep", bufs=1))
+        psum = ctx.enter_context(tc.psum_pool(name="psum", bufs=1))
+
+        def load_list(name, src):
+            t = lists.tile(list(src.shape), U16, name=name)
+            nc.sync.dma_start(t[:], src)
+            return t
+
+        def zeroed_bytes(name, width):
+            t = keep.tile([P, width], U8, name=name, align_bytes=64)
+            nc.vector.memset(t[:].bitcast(I32), 0)
+            return t
+
+        def place_scale_rows(dst, src):
+            for r in range(4):
+                nc.sync.dma_start(dst[r:P:32, :].bitcast(I32), src[8 * r:P:32, :].bitcast(I32))
+
+        def deal_words(name, src):
+            t = keep.tile([P, S], U32, name=name, align_bytes=64)
+            nc.vector.tensor_copy(
+                t[:].rearrange("p (t c i) -> p c t i", t=PACK, i=4),
+                src[:].rearrange("p (c i t) -> p c t i", t=PACK, i=4),
+            )
+            return t
+
+        def deal_bytes(name, src, planes):
+            t = keep.tile([P, planes * S], U8, name=name, align_bytes=64)
+            nc.vector.tensor_copy(
+                t[:].rearrange("p (a t m) -> p a t m", a=planes, t=PACK),
+                src[:].rearrange("p (a m t) -> p a t m", a=planes, t=PACK),
+            )
+            return t
+
+        def gather_words(name, window, offsets):
+            t = keep.tile([P, S], U32, name=name, align_bytes=64)
+            nc.vector.tensor_copy(t[:], window[:].indirect(offsets[:]))
+            return t
+
+        d_byte_win = zeroed_bytes("d_byte_win", G)
+        x_byte_win = zeroed_bytes("x_byte_win", T)
+        d_plane = zeroed_bytes("d_plane", 3 * S)
+        x_plane = zeroed_bytes("x_plane", 3 * S)
+        c_rows = zeroed_bytes("c_rows", S)
+        nc.sync.dma_start(d_byte_win[0:P:8, :].bitcast(I32), d_scales[0].bitcast(I32))
+        l_k1 = load_list("l_k1", k1)
+        l_k2 = load_list("l_k2", k2)
+        l_k3 = load_list("l_k3", k3)
+        nc.sync.dma_start(x_byte_win[0:P:8, :].bitcast(I32), x_scales[0].bitcast(I32))
+        l_offs = load_list("l_offs", offs)
+        l_two = load_list("l_two", two)
+        l_hz = load_list("l_hz", hz)
+        d_word_win = keep.tile([P, G], U32, name="d_word_win")
+        nc.sync.dma_start(d_word_win[:].bitcast(I32), d_words[0].rearrange("p n t -> p (n t)").bitcast(I32))
+        x_word_win = keep.tile([P, T], U32, name="x_word_win")
+        nc.sync.dma_start(x_word_win[:].bitcast(I32), x_words[0].rearrange("p n t -> p (n t)").bitcast(I32))
+        gain = keep.tile([P, PACK], F32, name="gain")
+        nc.sync.dma_start(gain[:], gs.rearrange("(p t) o -> p (t o)", t=PACK))
+        l_cand = load_list("l_cand", cand)
+        l_n2 = load_list("l_n2", n2)
+        l_n1 = load_list("l_n1", n1)
+        l_n3 = load_list("l_n3", n3)
+        l_n4 = load_list("l_n4", n4)
+        l_n5 = load_list("l_n5", n5)
+        gain16 = keep.tile([P, PACK], F32, name="gain16")
+        nc.scalar.activation(gain16[:], gain[:], COPY, scale=SIXTEENTH)
+
+        d_bytes = keep.tile([P, 3 * S], U8, name="d_bytes", align_bytes=64)
+        for a, lst in enumerate((l_k1, l_k2, l_k3)):
+            nc.vector.tensor_copy(d_bytes[:, a * S:(a + 1) * S], d_byte_win[:].indirect(lst[:]))
+        d_bytes_dealt = deal_bytes("d_bytes_dealt", d_bytes, 3)
+        place_scale_rows(d_plane, d_bytes_dealt)
+        x_bytes = keep.tile([P, 3 * S], U8, name="x_bytes", align_bytes=64)
+        for a, lst in enumerate((l_offs, l_two, l_hz)):
+            nc.vector.tensor_copy(x_bytes[:, a * S:(a + 1) * S], x_byte_win[:].indirect(lst[:]))
+        place_scale_rows(x_plane, x_bytes)
+        l_n8 = load_list("l_n8", n8)
+        l_n6 = load_list("l_n6", n6)
+        l_n7 = load_list("l_n7", n7)
+
+        h_bank = [psum.tile([P, S], F32, name="h_bank%d" % t, tag="bank%d" % t) for t in range(PACK)]
+        for a, (dl, xl) in enumerate(((l_k1, l_offs), (l_k2, l_two), (l_k3, l_hz))):
+            dw = deal_words("d_dealt%d" % a, gather_words("d_picked%d" % a, d_word_win, dl))
+            xw = gather_words("x_picked%d" % a, x_word_win, xl)
+            for t in range(PACK):
+                nc.tensor.matmul_mx(
+                    out=h_bank[t][:],
+                    lhsT=dw[:, t * P:(t + 1) * P].bitcast(FP8X4),
+                    lhsT_scale=d_plane[:, a * S + t * P:a * S + (t + 1) * P],
+                    rhs=xw[:].bitcast(FP8X4),
+                    rhs_scale=x_plane[:, a * S:(a + 1) * S],
+                    start=(a == 0),
+                    stop=(a == 2),
+                )
+
+        c_bytes = keep.tile([P, S], U8, name="c_bytes", align_bytes=64)
+        nc.vector.tensor_copy(c_bytes[:], x_byte_win[:].indirect(l_cand[:]))
+        place_scale_rows(c_rows, c_bytes)
+        c_picked = gather_words("c_picked", x_word_win, l_cand)
+
+        pa, pb, rb, ub, h5 = {}, {}, {}, {}, {}
+        z_rows = keep.tile([P, PACK, S], BF16, name="z_rows")
+
+        def fetch_pairs(t):
+            h = keep.tile([P, S], F32, name="h%d" % t)
+            nc.scalar.activation(h[:], h_bank[t][:], COPY, scale=SIXTEENTH)
+            pb[t] = keep.tile([P, W], F32, name="pb%d" % t)
+            nc.scalar.activation(pb[t][:], h[:].indirect(l_n2[:]), COPY)
+            pa[t] = keep.tile([P, W], F32, name="pa%d" % t)
+            nc.scalar.activation(pa[t][:], h[:].indirect(l_n1[:]), COPY)
+
+        def fetch_n5(t):
+            hg = keep.tile([P, S], F32, name="hg%d" % t)
+            nc.scalar.activation(hg[:], h_bank[t][:], COPY, scale=gain16[:, t:t + 1])
+            h5[t] = keep.tile([P, S], F32, name="h5_%d" % t)
+            for u in range(2):
+                nc.scalar.activation(h5[t][:, u * W:(u + 1) * W], hg[:].indirect(l_n5[:, u * 16:(u + 1) * 16]), COPY)
+
+        def finish_z(t):
+            nc.vector.scalar_tensor_tensor(z_rows[:, t, :], ub[t][:], gain[:, t:t + 1], h5[t][:], ALU.mult, ALU.subtract)
+
+        fetch_pairs(0)
+        for t in range(PACK):
+            if t + 1 < PACK:
+                fetch_pairs(t + 1)
+            fetch_n5(t)
+        for t in range(PACK):
+            rb[t] = keep.tile([P, W], F32, name="rb%d" % t)
+            ub[t] = keep.tile([P, S], F32, name="ub%d" % t)
+            nc.vector.tensor_copy(ub[t][:].indirect(l_n3[:]), pb[t][:])
+            nc.vector.tensor_tensor(rb[t][:], pa[t][:], pb[t][:], ALU.max)
+            if t > 0:
+                finish_z(t - 1)
+            nc.vector.tensor_copy(ub[t][:].indirect(l_n4[:]), rb[t][:])
+        c_dealt = deal_words("c_dealt", c_picked)
+        finish_z(PACK - 1)
+        c_plane = deal_bytes("c_plane", c_rows, 1)
+
+        z_words = keep.tile([P, S], U32, name="z_words", align_bytes=64)
+        z_plane = keep.tile([P, S], U8, name="z_plane", align_bytes=64)
+        s = [keep.tile([P, S], F32, name="s%d" % t) for t in range(PACK)]
+        both = [keep.tile([P, 2 * S], F32, name="both%d" % t) for t in range(PACK)]
+        page = [keep.tile([P, U], F32, name="page%d" % t) for t in range(PACK)]
+
+        def score(bank, t, cols):
+            nc.tensor.matmul_mx(
+                out=bank,
+                lhsT=c_dealt[:, t * P:(t + 1) * P].bitcast(FP8X4),
+                lhsT_scale=c_plane[:, t * P:(t + 1) * P],
+                rhs=z_words[:, cols].bitcast(FP8X4),
+                rhs_scale=z_plane[:, cols],
+                start=True,
+                stop=True,
+            )
+            nc.scalar.activation(s[t][:, cols], bank, COPY, scale=SIXTEENTH)
+
+        for c in range(S // CHUNK):
+            cols = slice(c * CHUNK, (c + 1) * CHUNK)
+            woven = keep.tile([P, CHUNK * PACK], BF16, name="woven%d" % c, align_bytes=64)
+            dst = woven[:].rearrange("p (c i t) -> p c t i", t=PACK, i=4)
+            src = z_rows[:, :, cols].rearrange("p t (c i) -> p c t i", i=4)
+            if c == 0:
+                nc.vector.tensor_copy(dst, src)
+            else:
+                nc.scalar.copy(dst, src)
+            nc.vector.quantize_mx(out=z_words[:, cols].bitcast(FP8X4), scales=z_plane[:, cols], in_=woven[:])
+            bank = psum.tile([P, CHUNK], F32, name="s0_bank%d" % c, tag="bank%d" % c)
+            score(bank[:], 0, cols)
+        for c in range(S // CHUNK):
+            cols = slice(c * CHUNK, (c + 1) * CHUNK)
+            nc.vector.tensor_copy(both[0][:].indirect(l_n8[:, c * 8:(c + 1) * 8]), s[0][:, cols])
+        for t in range(1, PACK):
+            bank = psum.tile([P, S], F32, name="s_bank%d" % t)
+            score(bank[:], t, slice(0, S))
+
+        out_rows = out.rearrange("(p t) w -> t p w", t=PACK)
+        for t in range(PACK):
+            nc.vector.tensor_tensor(both[t][:, S:], s[t][:], both[t][:, :S], ALU.max)
+            nc.vector.tensor_copy(page[t][:].indirect(l_n6[:]), both[t][:, :S])
+            if t + 1 < PACK:
+                nc.vector.tensor_copy(both[t + 1][:].indirect(l_n8[:]), s[t + 1][:])
+            nc.vector.tensor_copy(page[t][:].indirect(l_n7[:]), both[t][:, S:])
+            nc.sync.dma_start(out_rows[t], page[t][:])

@@ -1,6 +1,7 @@
 from contextlib import ExitStack
 
 import concourse.mybir as mybir
+from concourse.masks import make_identity
 
 F32 = mybir.dt.float32
 BF16 = mybir.dt.bfloat16
@@ -11,6 +12,7 @@ U8 = mybir.dt.uint8
 FP8X4 = mybir.dt.float8_e4m3fn_x4
 ALU = mybir.AluOpType
 COPY = mybir.ActivationFunctionType.Copy
+RELU = mybir.ActivationFunctionType.Relu
 
 P = 128
 PACK = 4
@@ -28,6 +30,7 @@ def tile_picked_mtthzkcpswpagsn_none_p_kernel(
     with ExitStack() as ctx:
         lists = ctx.enter_context(tc.tile_pool(name="lists", bufs=1))
         keep = ctx.enter_context(tc.tile_pool(name="keep", bufs=1))
+        chain = ctx.enter_context(tc.tile_pool(name="chain", bufs=1))
         psum = ctx.enter_context(tc.psum_pool(name="psum", bufs=1))
 
         def load_list(name, src):
@@ -35,41 +38,43 @@ def tile_picked_mtthzkcpswpagsn_none_p_kernel(
             nc.sync.dma_start(t[:], src)
             return t
 
-        def zeroed_bytes(name, width):
-            t = keep.tile([P, width], U8, name=name, align_bytes=64)
+        def zeroed_bytes(name, width, tag=""):
+            t = keep.tile([P, width], U8, name=name, align_bytes=64, tag=tag)
             nc.vector.memset(t[:].bitcast(I32), 0)
             return t
 
-        def place_scale_rows(dst, src):
-            for r in range(4):
-                nc.sync.dma_start(dst[r:P:32, :].bitcast(I32), src[8 * r:P:32, :].bitcast(I32))
+        def place_scale_rows(dst, first, src, cols):
+            for q in range(0, P, 32):
+                nc.sync.dma_start(dst[q + first:q + first + 4, :].bitcast(I32), src[q:q + 32:8, cols].bitcast(I32))
 
-        def deal_words(name, src):
-            t = keep.tile([P, S], U32, name=name, align_bytes=64)
+        def deal_words(name, src, tag=""):
+            t = keep.tile([P, S], U32, name=name, align_bytes=64, tag=tag)
             nc.vector.tensor_copy(
                 t[:].rearrange("p (t c i) -> p c t i", t=PACK, i=4),
                 src[:].rearrange("p (c i t) -> p c t i", t=PACK, i=4),
             )
             return t
 
-        def deal_bytes(name, src, planes):
-            t = keep.tile([P, planes * S], U8, name=name, align_bytes=64)
+        def deal_bytes(name, src, planes, tag=""):
+            t = keep.tile([P, planes * S], U8, name=name, align_bytes=64, tag=tag)
             nc.vector.tensor_copy(
                 t[:].rearrange("p (a t m) -> p a t m", a=planes, t=PACK),
                 src[:].rearrange("p (a m t) -> p a t m", a=planes, t=PACK),
             )
             return t
 
-        def gather_words(name, window, offsets):
-            t = keep.tile([P, S], U32, name=name, align_bytes=64)
+        def gather_words(name, window, offsets, offset):
+            t = chain.tile([P, S], U32, name=name, align_bytes=64, offset=offset)
             nc.vector.tensor_copy(t[:], window[:].indirect(offsets[:]))
             return t
 
         d_byte_win = zeroed_bytes("d_byte_win", G)
         x_byte_win = zeroed_bytes("x_byte_win", T)
-        d_plane = zeroed_bytes("d_plane", 3 * S)
+        d_rows = zeroed_bytes("d_rows", S, "d_dealt2")
         x_plane = zeroed_bytes("x_plane", 3 * S)
         c_rows = zeroed_bytes("c_rows", S)
+        ident = keep.tile([P, P], F32, name="ident")
+        make_identity(nc, ident[:])
         nc.sync.dma_start(d_byte_win[0:P:8, :].bitcast(I32), d_scales[0].bitcast(I32))
         l_k1 = load_list("l_k1", k1)
         l_k2 = load_list("l_k2", k2)
@@ -78,95 +83,110 @@ def tile_picked_mtthzkcpswpagsn_none_p_kernel(
         l_offs = load_list("l_offs", offs)
         l_two = load_list("l_two", two)
         l_hz = load_list("l_hz", hz)
-        d_word_win = keep.tile([P, G], U32, name="d_word_win")
-        nc.sync.dma_start(d_word_win[:].bitcast(I32), d_words[0].rearrange("p n t -> p (n t)").bitcast(I32))
-        x_word_win = keep.tile([P, T], U32, name="x_word_win")
-        nc.sync.dma_start(x_word_win[:].bitcast(I32), x_words[0].rearrange("p n t -> p (n t)").bitcast(I32))
-        gain = keep.tile([P, PACK], F32, name="gain")
-        nc.sync.dma_start(gain[:], gs.rearrange("(p t) o -> p (t o)", t=PACK))
         l_cand = load_list("l_cand", cand)
         l_n2 = load_list("l_n2", n2)
+        x_word_win = keep.tile([P, T], U32, name="x_word_win")
+        nc.sync.dma_start(x_word_win[:].bitcast(I32), x_words[0].rearrange("p n t -> p (n t)").bitcast(I32))
+        d_word_win = keep.tile([P, G], U32, name="d_word_win")
+        nc.sync.dma_start(d_word_win[:].bitcast(I32), d_words[0].rearrange("p n t -> p (n t)").bitcast(I32))
+
+        for a, lst in enumerate((l_k1, l_k2, l_k3)):
+            d_bytes = keep.tile([P, S], U8, name="d_bytes%d" % a, align_bytes=64)
+            nc.vector.tensor_copy(d_bytes[:], d_byte_win[:].indirect(lst[:]))
+            place_scale_rows(d_rows, 4 * a, d_bytes, slice(0, S))
+        x_bytes = keep.tile([P, 3 * S], U8, name="x_bytes", align_bytes=64)
+        for a, lst in enumerate((l_offs, l_two, l_hz)):
+            nc.vector.tensor_copy(x_bytes[:, a * S:(a + 1) * S], x_byte_win[:].indirect(lst[:]))
+        place_scale_rows(x_plane, 0, x_bytes, slice(0, 3 * S))
+        d_plane = deal_bytes("d_plane", d_rows, 1)
+        gain = keep.tile([P, PACK], F32, name="gain")
+        nc.sync.dma_start(gain[:], gs.rearrange("(p t) o -> p (t o)", t=PACK))
         l_n1 = load_list("l_n1", n1)
         l_n3 = load_list("l_n3", n3)
         l_n4 = load_list("l_n4", n4)
         l_n5 = load_list("l_n5", n5)
-        gain16 = keep.tile([P, PACK], F32, name="gain16")
-        nc.scalar.activation(gain16[:], gain[:], COPY, scale=SIXTEENTH)
-
-        d_bytes = keep.tile([P, 3 * S], U8, name="d_bytes", align_bytes=64)
-        for a, lst in enumerate((l_k1, l_k2, l_k3)):
-            nc.vector.tensor_copy(d_bytes[:, a * S:(a + 1) * S], d_byte_win[:].indirect(lst[:]))
-        d_bytes_dealt = deal_bytes("d_bytes_dealt", d_bytes, 3)
-        place_scale_rows(d_plane, d_bytes_dealt)
-        x_bytes = keep.tile([P, 3 * S], U8, name="x_bytes", align_bytes=64)
-        for a, lst in enumerate((l_offs, l_two, l_hz)):
-            nc.vector.tensor_copy(x_bytes[:, a * S:(a + 1) * S], x_byte_win[:].indirect(lst[:]))
-        place_scale_rows(x_plane, x_bytes)
         l_n8 = load_list("l_n8", n8)
         l_n6 = load_list("l_n6", n6)
         l_n7 = load_list("l_n7", n7)
 
-        h_bank = [psum.tile([P, S], F32, name="h_bank%d" % t, tag="bank%d" % t) for t in range(PACK)]
+
+        d_at = (8192, 10240, 1984)
+        x_at = (12288, 14336, 0)
+        dw, xw = [], []
         for a, (dl, xl) in enumerate(((l_k1, l_offs), (l_k2, l_two), (l_k3, l_hz))):
-            dw = deal_words("d_dealt%d" % a, gather_words("d_picked%d" % a, d_word_win, dl))
-            xw = gather_words("x_picked%d" % a, x_word_win, xl)
-            for t in range(PACK):
+            dw.append(deal_words("d_dealt%d" % a, gather_words("d_picked%d" % a, d_word_win, dl, d_at[a]), "d_dealt%d" % a))
+            xw.append(gather_words("x_picked%d" % a, x_word_win, xl, x_at[a]))
+        h = {}
+
+        def first_product(t):
+            bank = psum.tile([P, S], F32, name="h_bank%d" % t, tag="h_bank")
+            for a in range(3):
                 nc.tensor.matmul_mx(
-                    out=h_bank[t][:],
-                    lhsT=dw[:, t * P:(t + 1) * P].bitcast(FP8X4),
-                    lhsT_scale=d_plane[:, a * S + t * P:a * S + (t + 1) * P],
-                    rhs=xw[:].bitcast(FP8X4),
+                    out=bank[:],
+                    lhsT=dw[a][:, t * P:(t + 1) * P].bitcast(FP8X4),
+                    lhsT_scale=d_plane[4 * a:P, t * P:(t + 1) * P],
+                    rhs=xw[a][:].bitcast(FP8X4),
                     rhs_scale=x_plane[:, a * S:(a + 1) * S],
                     start=(a == 0),
                     stop=(a == 2),
                 )
+            h[t] = keep.tile([P, S], F32, name="h%d" % t)
+            nc.scalar.activation(h[t][:], bank[:], COPY, scale=SIXTEENTH)
 
-        c_bytes = keep.tile([P, S], U8, name="c_bytes", align_bytes=64)
+        c_bytes = chain.tile([P, S], U8, name="c_bytes", align_bytes=64, offset=2048)
         nc.vector.tensor_copy(c_bytes[:], x_byte_win[:].indirect(l_cand[:]))
-        place_scale_rows(c_rows, c_bytes)
-        c_picked = gather_words("c_picked", x_word_win, l_cand)
+        place_scale_rows(c_rows, 0, c_bytes, slice(0, S))
+        c_picked = gather_words("c_picked", x_word_win, l_cand, 2560)
 
         pa, pb, rb, ub, h5 = {}, {}, {}, {}, {}
         z_rows = keep.tile([P, PACK, S], BF16, name="z_rows")
 
-        def fetch_pairs(t):
-            h = keep.tile([P, S], F32, name="h%d" % t)
-            nc.scalar.activation(h[:], h_bank[t][:], COPY, scale=SIXTEENTH)
-            pb[t] = keep.tile([P, W], F32, name="pb%d" % t)
-            nc.scalar.activation(pb[t][:], h[:].indirect(l_n2[:]), COPY)
-            pa[t] = keep.tile([P, W], F32, name="pa%d" % t)
-            nc.scalar.activation(pa[t][:], h[:].indirect(l_n1[:]), COPY)
+        hg = {}
 
-        def fetch_n5(t):
-            hg = keep.tile([P, S], F32, name="hg%d" % t)
-            nc.scalar.activation(hg[:], h_bank[t][:], COPY, scale=gain16[:, t:t + 1])
-            h5[t] = keep.tile([P, S], F32, name="h5_%d" % t)
-            for u in range(2):
-                nc.scalar.activation(h5[t][:, u * W:(u + 1) * W], hg[:].indirect(l_n5[:, u * 16:(u + 1) * 16]), COPY)
+        def unload_weighted(t):
+            hg[t] = keep.tile([P, S], F32, name="hg%d" % t)
+            nc.scalar.activation(hg[t][:], h[t][:], COPY, scale=gain[:, t:t + 1])
+            h5[t] = keep.tile([P, S], F32, name="h5_%d" % t, align_bytes=64, tag="h5_%d" % t)
+
+        def fetch(dst, name, t, lst):
+            dst[t] = keep.tile([P, W], F32, name="%s%d" % (name, t), align_bytes=64, tag="%s%d" % (name, t))
+            nc.scalar.activation(dst[t][:], h[t][:].indirect(lst[:]), COPY)
+
+        def fetch_n5(t, u):
+            nc.scalar.activation(h5[t][:, u * W:(u + 1) * W], hg[t][:].indirect(l_n5[:, u * 16:(u + 1) * 16]), COPY)
 
         def finish_z(t):
             nc.vector.scalar_tensor_tensor(z_rows[:, t, :], ub[t][:], gain[:, t:t + 1], h5[t][:], ALU.mult, ALU.subtract)
 
-        fetch_pairs(0)
-        for t in range(PACK):
-            if t + 1 < PACK:
-                fetch_pairs(t + 1)
-            fetch_n5(t)
+        first_product(0)
+        fetch(pb, "pb", 0, l_n2)
+        fetch(pa, "pa", 0, l_n1)
+        for t in range(1, PACK):
+            first_product(t)
+            unload_weighted(t - 1)
+            fetch_n5(t - 1, 0)
+            fetch(pa, "pa", t, l_n1)
+            fetch(pb, "pb", t, l_n2)
+            fetch_n5(t - 1, 1)
+        unload_weighted(PACK - 1)
+        fetch_n5(PACK - 1, 0)
+        fetch_n5(PACK - 1, 1)
         for t in range(PACK):
             rb[t] = keep.tile([P, W], F32, name="rb%d" % t)
             ub[t] = keep.tile([P, S], F32, name="ub%d" % t)
-            nc.vector.tensor_copy(ub[t][:].indirect(l_n3[:]), pb[t][:])
             nc.vector.tensor_tensor(rb[t][:], pa[t][:], pb[t][:], ALU.max)
+            nc.vector.tensor_copy(ub[t][:].indirect(l_n3[:]), pb[t][:])
             if t > 0:
                 finish_z(t - 1)
             nc.vector.tensor_copy(ub[t][:].indirect(l_n4[:]), rb[t][:])
-        c_dealt = deal_words("c_dealt", c_picked)
+        c_dealt = deal_words("c_dealt", c_picked, "pb3")
         finish_z(PACK - 1)
-        c_plane = deal_bytes("c_plane", c_rows, 1)
+        c_plane = deal_bytes("c_plane", c_rows, 1, "pa3")
 
         z_words = keep.tile([P, S], U32, name="z_words", align_bytes=64)
         z_plane = keep.tile([P, S], U8, name="z_plane", align_bytes=64)
         s = [keep.tile([P, S], F32, name="s%d" % t) for t in range(PACK)]
+        neg_s = [keep.tile([P, S], F32, name="neg_s%d" % t) for t in range(PACK)]
         both = [keep.tile([P, 2 * S], F32, name="both%d" % t) for t in range(PACK)]
         page = [keep.tile([P, U], F32, name="page%d" % t) for t in range(PACK)]
 
@@ -180,14 +200,17 @@ def tile_picked_mtthzkcpswpagsn_none_p_kernel(
                 start=True,
                 stop=True,
             )
-            nc.scalar.activation(s[t][:, cols], bank, COPY, scale=SIXTEENTH)
+            if t == 0 and cols.start == 0:
+                nc.vector.tensor_scalar(s[t][:, cols], bank, SIXTEENTH, None, ALU.mult)
+            else:
+                nc.scalar.activation(s[t][:, cols], bank, COPY, scale=SIXTEENTH)
 
         for c in range(S // CHUNK):
             cols = slice(c * CHUNK, (c + 1) * CHUNK)
             woven = keep.tile([P, CHUNK * PACK], BF16, name="woven%d" % c, align_bytes=64)
             dst = woven[:].rearrange("p (c i t) -> p c t i", t=PACK, i=4)
             src = z_rows[:, :, cols].rearrange("p t (c i) -> p c t i", i=4)
-            if c == 0:
+            if c < 2:
                 nc.vector.tensor_copy(dst, src)
             else:
                 nc.scalar.copy(dst, src)
@@ -201,11 +224,26 @@ def tile_picked_mtthzkcpswpagsn_none_p_kernel(
             bank = psum.tile([P, S], F32, name="s_bank%d" % t)
             score(bank[:], t, slice(0, S))
 
+        def excess(t):
+            nc.scalar.activation(neg_s[t][:], s[t][:], COPY, scale=-1.0)
+            turned = psum.tile([P, S], F32, name="turned%d" % t, tag="bank%d" % (2 * t % 4))
+            for c in range(S // P):
+                cols = slice(c * P, (c + 1) * P)
+                nc.tensor.matmul(turned[:, cols], neg_s[t][:, cols], ident[:], start=True, stop=False, is_transpose=True)
+                nc.tensor.matmul(turned[:, cols], both[t][:, cols], ident[:], start=False, stop=True, is_transpose=True)
+            pos = keep.tile([P, S], F32, name="pos%d" % t)
+            nc.scalar.activation(pos[:], turned[:], RELU)
+            back = psum.tile([P, S], F32, name="back%d" % t, tag="bank%d" % ((2 * t + 1) % 4))
+            for c in range(S // P):
+                cols = slice(c * P, (c + 1) * P)
+                nc.tensor.transpose(back[:, cols], pos[:, cols], ident[:])
+            nc.scalar.activation(both[t][:, S:], back[:], COPY)
+
         out_rows = out.rearrange("(p t) w -> t p w", t=PACK)
         for t in range(PACK):
-            nc.vector.tensor_tensor(both[t][:, S:], s[t][:], both[t][:, :S], ALU.max)
+            excess(t)
             nc.vector.tensor_copy(page[t][:].indirect(l_n6[:]), both[t][:, :S])
             if t + 1 < PACK:
                 nc.vector.tensor_copy(both[t + 1][:].indirect(l_n8[:]), s[t + 1][:])
-            nc.vector.tensor_copy(page[t][:].indirect(l_n7[:]), both[t][:, S:])
+            nc.vector.tensor_tensor(page[t][:].indirect(l_n7[:]), both[t][:, S:], s[t][:], ALU.add)
             nc.sync.dma_start(out_rows[t], page[t][:])

@@ -70,11 +70,12 @@ def tile_picked_mtthzkcpswpagsn_none_p_kernel(
 
         d_byte_win = zeroed_bytes("d_byte_win", G)
         x_byte_win = zeroed_bytes("x_byte_win", T)
+        ident = keep.tile([P, P], F32, name="ident")
+        nc.vector.memset(ident[:], 0.0)
+        make_identity(nc, ident[:], nomemset=True)
         d_rows = zeroed_bytes("d_rows", S, "d_dealt2")
         x_plane = zeroed_bytes("x_plane", 3 * S)
         c_rows = zeroed_bytes("c_rows", S)
-        ident = keep.tile([P, P], F32, name="ident")
-        make_identity(nc, ident[:])
         nc.sync.dma_start(d_byte_win[0:P:8, :].bitcast(I32), d_scales[0].bitcast(I32))
         l_k1 = load_list("l_k1", k1)
         l_k2 = load_list("l_k2", k2)
@@ -155,8 +156,10 @@ def tile_picked_mtthzkcpswpagsn_none_p_kernel(
         def fetch_n5(t, u):
             nc.scalar.activation(h5[t][:, u * W:(u + 1) * W], hg[t][:].indirect(l_n5[:, u * 16:(u + 1) * 16]), COPY)
 
-        def finish_z(t):
-            nc.vector.scalar_tensor_tensor(z_rows[:, t, :], ub[t][:], gain[:, t:t + 1], h5[t][:], ALU.mult, ALU.subtract)
+        def finish_z(t, cols=slice(0, S)):
+            nc.vector.scalar_tensor_tensor(
+                z_rows[:, t, cols], ub[t][:, cols], gain[:, t:t + 1], h5[t][:, cols], ALU.mult, ALU.subtract
+            )
 
         first_product(0)
         fetch(pb, "pb", 0, l_n2)
@@ -180,8 +183,8 @@ def tile_picked_mtthzkcpswpagsn_none_p_kernel(
                 finish_z(t - 1)
             nc.vector.tensor_copy(ub[t][:].indirect(l_n4[:]), rb[t][:])
         c_dealt = deal_words("c_dealt", c_picked, "pb3")
-        finish_z(PACK - 1)
-        c_plane = deal_bytes("c_plane", c_rows, 1, "pa3")
+        finish_z(PACK - 1, slice(0, CHUNK))
+        finish_z(PACK - 1, slice(CHUNK, S))
 
         z_words = keep.tile([P, S], U32, name="z_words", align_bytes=64)
         z_plane = keep.tile([P, S], U8, name="z_plane", align_bytes=64)
@@ -205,21 +208,22 @@ def tile_picked_mtthzkcpswpagsn_none_p_kernel(
             else:
                 nc.scalar.activation(s[t][:, cols], bank, COPY, scale=SIXTEENTH)
 
-        for c in range(S // CHUNK):
-            cols = slice(c * CHUNK, (c + 1) * CHUNK)
-            woven = keep.tile([P, CHUNK * PACK], BF16, name="woven%d" % c, align_bytes=64)
+        for c, cols in enumerate((slice(0, CHUNK), slice(CHUNK, 2 * CHUNK), slice(2 * CHUNK, S))):
+            width = cols.stop - cols.start
+            woven = keep.tile([P, width * PACK], BF16, name="woven%d" % c, align_bytes=64)
             dst = woven[:].rearrange("p (c i t) -> p c t i", t=PACK, i=4)
             src = z_rows[:, :, cols].rearrange("p t (c i) -> p c t i", i=4)
-            if c < 2:
+            if c != 1:
                 nc.vector.tensor_copy(dst, src)
             else:
                 nc.scalar.copy(dst, src)
+            if c == 0:
+                c_plane = deal_bytes("c_plane", c_rows, 1, "h5_3")
             nc.vector.quantize_mx(out=z_words[:, cols].bitcast(FP8X4), scales=z_plane[:, cols], in_=woven[:])
-            bank = psum.tile([P, CHUNK], F32, name="s0_bank%d" % c, tag="bank%d" % c)
+            bank = psum.tile([P, width], F32, name="s0_bank%d" % c, tag="bank%d" % c)
             score(bank[:], 0, cols)
-        for c in range(S // CHUNK):
-            cols = slice(c * CHUNK, (c + 1) * CHUNK)
-            nc.vector.tensor_copy(both[0][:].indirect(l_n8[:, c * 8:(c + 1) * 8]), s[0][:, cols])
+        for cols in (slice(0, CHUNK), slice(CHUNK, S)):
+            nc.vector.tensor_copy(both[0][:].indirect(l_n8[:, cols.start // 16:cols.stop // 16]), s[0][:, cols])
         for t in range(1, PACK):
             bank = psum.tile([P, S], F32, name="s_bank%d" % t)
             score(bank[:], t, slice(0, S))

from contextlib import ExitStack

import concourse.mybir as mybir
from concourse.masks import make_identity

F32 = mybir.dt.float32
BF16 = mybir.dt.bfloat16
I32 = mybir.dt.int32
U32 = mybir.dt.uint32
U16 = mybir.dt.uint16
U8 = mybir.dt.uint8
FP8X4 = mybir.dt.float8_e4m3fn_x4
ALU = mybir.AluOpType
COPY = mybir.ActivationFunctionType.Copy
RELU = mybir.ActivationFunctionType.Relu

P = 128
PACK = 4
T, G, S, W, U = 1024, 2048, 512, 256, 1024
CHUNK = 128
SIXTEENTH = 0.0625
FLOPS = 4 * 2 * 512 * 512 * 512


def tile_picked_mtthzkcpswpagsn_none_p_kernel(
    tc, x_words, x_scales, d_words, d_scales, gs, offs, k1, two, k2, hz, k3,
    n1, n2, n3, n4, n5, cand, n6, n7, n8, out,
):
    nc = tc.nc
    with ExitStack() as ctx:
        lists = ctx.enter_context(tc.tile_pool(name="lists", bufs=1))
        keep = ctx.enter_context(tc.tile_pool(name="keep", bufs=1))
        chain = ctx.enter_context(tc.tile_pool(name="chain", bufs=1))
        psum = ctx.enter_context(tc.psum_pool(name="psum", bufs=1))

        def load_list(name, src):
            t = lists.tile(list(src.shape), U16, name=name)
            nc.sync.dma_start(t[:], src)
            return t

        def zeroed_bytes(name, width, tag=""):
            t = keep.tile([P, width], U8, name=name, align_bytes=64, tag=tag)
            nc.vector.memset(t[:].bitcast(I32), 0)
            return t

        def place_scale_rows(dst, first, src, cols):
            for q in range(0, P, 32):
                nc.sync.dma_start(dst[q + first:q + first + 4, :].bitcast(I32), src[q:q + 32:8, cols].bitcast(I32))

        def deal_words(name, src, tag=""):
            t = keep.tile([P, S], U32, name=name, align_bytes=64, tag=tag)
            nc.vector.tensor_copy(
                t[:].rearrange("p (t c i) -> p c t i", t=PACK, i=4),
                src[:].rearrange("p (c i t) -> p c t i", t=PACK, i=4),
            )
            return t

        def deal_bytes(name, src, planes, tag=""):
            t = keep.tile([P, planes * S], U8, name=name, align_bytes=64, tag=tag)
            nc.vector.tensor_copy(
                t[:].rearrange("p (a t m) -> p a t m", a=planes, t=PACK),
                src[:].rearrange("p (a m t) -> p a t m", a=planes, t=PACK),
            )
            return t

        def gather_words(name, window, offsets, offset):
            t = chain.tile([P, S], U32, name=name, align_bytes=64, offset=offset)
            nc.vector.tensor_copy(t[:], window[:].indirect(offsets[:]))
            return t

        d_byte_win = zeroed_bytes("d_byte_win", G)
        x_byte_win = zeroed_bytes("x_byte_win", T)
        ident = keep.tile([P, P], F32, name="ident")
        nc.vector.memset(ident[:], 0.0)
        make_identity(nc, ident[:], nomemset=True)
        d_rows = zeroed_bytes("d_rows", S, "d_dealt2")
        x_plane = zeroed_bytes("x_plane", 3 * S)
        c_rows = zeroed_bytes("c_rows", S)
        nc.sync.dma_start(d_byte_win[0:P:8, :].bitcast(I32), d_scales[0].bitcast(I32))
        l_k1 = load_list("l_k1", k1)
        l_k2 = load_list("l_k2", k2)
        l_k3 = load_list("l_k3", k3)
        nc.sync.dma_start(x_byte_win[0:P:8, :].bitcast(I32), x_scales[0].bitcast(I32))
        l_offs = load_list("l_offs", offs)
        l_two = load_list("l_two", two)
        l_hz = load_list("l_hz", hz)
        l_cand = load_list("l_cand", cand)
        l_n2 = load_list("l_n2", n2)
        x_word_win = keep.tile([P, T], U32, name="x_word_win")
        nc.sync.dma_start(x_word_win[:].bitcast(I32), x_words[0].rearrange("p n t -> p (n t)").bitcast(I32))
        d_word_win = keep.tile([P, G], U32, name="d_word_win")
        nc.sync.dma_start(d_word_win[:].bitcast(I32), d_words[0].rearrange("p n t -> p (n t)").bitcast(I32))

        for a, lst in enumerate((l_k1, l_k2, l_k3)):
            d_bytes = keep.tile([P, S], U8, name="d_bytes%d" % a, align_bytes=64)
            nc.vector.tensor_copy(d_bytes[:], d_byte_win[:].indirect(lst[:]))
            place_scale_rows(d_rows, 4 * a, d_bytes, slice(0, S))
        x_bytes = keep.tile([P, 3 * S], U8, name="x_bytes", align_bytes=64)
        for a, lst in enumerate((l_offs, l_two, l_hz)):
            nc.vector.tensor_copy(x_bytes[:, a * S:(a + 1) * S], x_byte_win[:].indirect(lst[:]))
        place_scale_rows(x_plane, 0, x_bytes, slice(0, 3 * S))
        d_plane = deal_bytes("d_plane", d_rows, 1)
        gain = keep.tile([P, PACK], F32, name="gain")
        nc.sync.dma_start(gain[:], gs.rearrange("(p t) o -> p (t o)", t=PACK))
        l_n1 = load_list("l_n1", n1)
        l_n3 = load_list("l_n3", n3)
        l_n4 = load_list("l_n4", n4)
        l_n5 = load_list("l_n5", n5)
        l_n8 = load_list("l_n8", n8)
        l_n6 = load_list("l_n6", n6)
        l_n7 = load_list("l_n7", n7)


        d_at = (8192, 10240, 1984)
        x_at = (12288, 14336, 0)
        dw, xw = [], []
        for a, (dl, xl) in enumerate(((l_k1, l_offs), (l_k2, l_two), (l_k3, l_hz))):
            dw.append(deal_words("d_dealt%d" % a, gather_words("d_picked%d" % a, d_word_win, dl, d_at[a]), "d_dealt%d" % a))
            xw.append(gather_words("x_picked%d" % a, x_word_win, xl, x_at[a]))
        h = {}

        def first_product(t):
            bank = psum.tile([P, S], F32, name="h_bank%d" % t, tag="h_bank")
            for a in range(3):
                nc.tensor.matmul_mx(
                    out=bank[:],
                    lhsT=dw[a][:, t * P:(t + 1) * P].bitcast(FP8X4),
                    lhsT_scale=d_plane[4 * a:P, t * P:(t + 1) * P],
                    rhs=xw[a][:].bitcast(FP8X4),
                    rhs_scale=x_plane[:, a * S:(a + 1) * S],
                    start=(a == 0),
                    stop=(a == 2),
                )
            h[t] = keep.tile([P, S], F32, name="h%d" % t)
            nc.scalar.activation(h[t][:], bank[:], COPY, scale=SIXTEENTH)

        c_bytes = chain.tile([P, S], U8, name="c_bytes", align_bytes=64, offset=2048)
        nc.vector.tensor_copy(c_bytes[:], x_byte_win[:].indirect(l_cand[:]))
        place_scale_rows(c_rows, 0, c_bytes, slice(0, S))
        c_picked = gather_words("c_picked", x_word_win, l_cand, 2560)

        pa, pb, rb, ub, h5 = {}, {}, {}, {}, {}
        z_rows = keep.tile([P, PACK, S], BF16, name="z_rows")

        hg = {}

        def unload_weighted(t):
            hg[t] = keep.tile([P, S], F32, name="hg%d" % t)
            nc.scalar.activation(hg[t][:], h[t][:], COPY, scale=gain[:, t:t + 1])
            h5[t] = keep.tile([P, S], F32, name="h5_%d" % t, align_bytes=64, tag="h5_%d" % t)

        def fetch(dst, name, t, lst):
            dst[t] = keep.tile([P, W], F32, name="%s%d" % (name, t), align_bytes=64, tag="%s%d" % (name, t))
            nc.scalar.activation(dst[t][:], h[t][:].indirect(lst[:]), COPY)

        def fetch_n5(t, u):
            nc.scalar.activation(h5[t][:, u * W:(u + 1) * W], hg[t][:].indirect(l_n5[:, u * 16:(u + 1) * 16]), COPY)

        def finish_z(t, cols=slice(0, S)):
            nc.vector.scalar_tensor_tensor(
                z_rows[:, t, cols], ub[t][:, cols], gain[:, t:t + 1], h5[t][:, cols], ALU.mult, ALU.subtract
            )

        first_product(0)
        fetch(pb, "pb", 0, l_n2)
        fetch(pa, "pa", 0, l_n1)
        for t in range(1, PACK):
            first_product(t)
            unload_weighted(t - 1)
            fetch_n5(t - 1, 0)
            fetch(pa, "pa", t, l_n1)
            fetch(pb, "pb", t, l_n2)
            fetch_n5(t - 1, 1)
        unload_weighted(PACK - 1)
        fetch_n5(PACK - 1, 0)
        fetch_n5(PACK - 1, 1)
        for t in range(PACK):
            rb[t] = keep.tile([P, W], F32, name="rb%d" % t)
            ub[t] = keep.tile([P, S], F32, name="ub%d" % t)
            nc.vector.tensor_tensor(rb[t][:], pa[t][:], pb[t][:], ALU.max)
            nc.vector.tensor_copy(ub[t][:].indirect(l_n3[:]), pb[t][:])
            if t > 0:
                finish_z(t - 1)
            nc.vector.tensor_copy(ub[t][:].indirect(l_n4[:]), rb[t][:])
        c_dealt = deal_words("c_dealt", c_picked, "pb3")
        finish_z(PACK - 1, slice(0, CHUNK))
        finish_z(PACK - 1, slice(CHUNK, S))

        z_words = keep.tile([P, S], U32, name="z_words", align_bytes=64)
        z_plane = keep.tile([P, S], U8, name="z_plane", align_bytes=64)
        s = [keep.tile([P, S], F32, name="s%d" % t) for t in range(PACK)]
        neg_s = [keep.tile([P, S], F32, name="neg_s%d" % t) for t in range(PACK)]
        both = [keep.tile([P, 2 * S], F32, name="both%d" % t) for t in range(PACK)]
        page = [keep.tile([P, U], F32, name="page%d" % t) for t in range(PACK)]

        def score(bank, t, cols):
            nc.tensor.matmul_mx(
                out=bank,
                lhsT=c_dealt[:, t * P:(t + 1) * P].bitcast(FP8X4),
                lhsT_scale=c_plane[:, t * P:(t + 1) * P],
                rhs=z_words[:, cols].bitcast(FP8X4),
                rhs_scale=z_plane[:, cols],
                start=True,
                stop=True,
            )
            if t == 0 and cols.start == 0:
                nc.vector.tensor_scalar(s[t][:, cols], bank, SIXTEENTH, None, ALU.mult)
            else:
                nc.scalar.activation(s[t][:, cols], bank, COPY, scale=SIXTEENTH)

        for c, cols in enumerate((slice(0, CHUNK), slice(CHUNK, 2 * CHUNK), slice(2 * CHUNK, S))):
            width = cols.stop - cols.start
            woven = keep.tile([P, width * PACK], BF16, name="woven%d" % c, align_bytes=64)
            dst = woven[:].rearrange("p (c i t) -> p c t i", t=PACK, i=4)
            src = z_rows[:, :, cols].rearrange("p t (c i) -> p c t i", i=4)
            if c != 1:
                nc.vector.tensor_copy(dst, src)
            else:
                nc.scalar.copy(dst, src)
            if c == 0:
                c_plane = deal_bytes("c_plane", c_rows, 1, "h5_3")
            nc.vector.quantize_mx(out=z_words[:, cols].bitcast(FP8X4), scales=z_plane[:, cols], in_=woven[:])
            bank = psum.tile([P, width], F32, name="s0_bank%d" % c, tag="bank%d" % c)
            score(bank[:], 0, cols)
        for cols in (slice(0, CHUNK), slice(CHUNK, S)):
            nc.vector.tensor_copy(both[0][:].indirect(l_n8[:, cols.start // 16:cols.stop // 16]), s[0][:, cols])
        for t in range(1, PACK):
            bank = psum.tile([P, S], F32, name="s_bank%d" % t)
            score(bank[:], t, slice(0, S))

        def excess(t):
            nc.scalar.activation(neg_s[t][:], s[t][:], COPY, scale=-1.0)
            turned = psum.tile([P, S], F32, name="turned%d" % t, tag="bank%d" % (2 * t % 4))
            for c in range(S // P):
                cols = slice(c * P, (c + 1) * P)
                nc.tensor.matmul(turned[:, cols], neg_s[t][:, cols], ident[:], start=True, stop=False, is_transpose=True)
                nc.tensor.matmul(turned[:, cols], both[t][:, cols], ident[:], start=False, stop=True, is_transpose=True)
            pos = keep.tile([P, S], F32, name="pos%d" % t)
            nc.scalar.activation(pos[:], turned[:], RELU)
            back = psum.tile([P, S], F32, name="back%d" % t, tag="bank%d" % ((2 * t + 1) % 4))
            for c in range(S // P):
                cols = slice(c * P, (c + 1) * P)
                nc.tensor.transpose(back[:, cols], pos[:, cols], ident[:])
            nc.scalar.activation(both[t][:, S:], back[:], COPY)

        out_rows = out.rearrange("(p t) w -> t p w", t=PACK)
        for t in range(PACK):
            excess(t)
            nc.vector.tensor_copy(page[t][:].indirect(l_n6[:]), both[t][:, :S])
            if t + 1 < PACK:
                nc.vector.tensor_copy(both[t + 1][:].indirect(l_n8[:]), s[t + 1][:])
            nc.vector.tensor_tensor(page[t][:].indirect(l_n7[:]), both[t][:, S:], s[t][:], ALU.add)
            nc.sync.dma_start(out_rows[t], page[t][:])
